import numpy as np
import ml_dtypes


def mxq(x, axis, fmt="e4m3"):
    dtype, down = {"e4m3": (ml_dtypes.float8_e4m3fn, 7), "e5m2": (ml_dtypes.float8_e5m2, 14)}[fmt]
    v = np.moveaxis(np.asarray(x, np.float32).astype(ml_dtypes.bfloat16).astype(np.float64), axis, -1)
    blocks = v.reshape(v.shape[:-1] + (-1, 32))
    amax = np.abs(blocks).max(-1, keepdims=True)
    byte = np.maximum(np.where(amax > 0, np.frexp(amax)[1] - 1 + 127, 0) - down, 1)
    scale = np.exp2(byte - 127.0)
    codes = (blocks / scale).astype(np.float32).astype(dtype).astype(np.float64)
    return np.moveaxis((codes * scale).reshape(v.shape), -1, axis)


WIDE = False


def mx_kscale(k):
    if not WIDE:
        return np.ones(k)
    levels = np.array([10, -10, 5, -5, 0])
    if k % 512:
        return np.exp2(np.random.permutation(np.resize(levels, k // 32))).repeat(32)
    a = np.empty((k // 512, 16))
    for p in range(k // 512):
        a[p, :8] = np.random.permutation(np.resize(levels, 8))
        for g in range(8):
            far = levels[np.abs(levels - a[p, g]) >= 10]
            a[p, g + 8] = far[np.random.randint(len(far))]
    return np.exp2(a.ravel()).repeat(32)


def f64(x):
    return np.asarray(x).astype(np.float64)


def striped(idx):
    return np.tile(idx.reshape(-1, 16).T, (8, 1)).astype(np.uint16)


def unstriped(offs):
    return offs[:16].T.reshape(-1).astype(np.int64)


E2M1 = np.array([0.0, 0.5, 1.0, 1.5, 2.0, 3.0, 4.0, 6.0, -0.0, -0.5, -1.0, -1.5, -2.0, -3.0, -4.0, -6.0])


def pack_weight(w, fmt):
    k, n = w.shape
    w = f64(np.asarray(w, np.float32).astype(ml_dtypes.bfloat16)).reshape(k // 32, 32, n)
    amax = np.abs(w).max(1)
    if fmt == "e4m3":
        byte = np.frexp(amax)[1] - 1 + 127 - 7
    else:
        mant, ex = np.frexp(amax / 6.0)
        byte = np.where(mant > 0.5, ex, ex - 1) + 127
    byte = np.clip(np.where(amax > 0, byte, 1), 1, 254)
    scaled = (w * np.exp2(127.0 - byte)[:, None, :]).reshape(k, n).astype(np.float32)
    by_word = np.ascontiguousarray(scaled.reshape(k // 512, 128, 4, n).transpose(0, 1, 3, 2))
    if fmt == "e4m3":
        words = by_word.astype(ml_dtypes.float8_e4m3fn).view(np.uint8)
    else:
        c = by_word.astype(ml_dtypes.float4_e2m1fn).view(np.uint8) & 0xF
        words = (c[..., 0::2] | (c[..., 1::2] << 4)).reshape(k // 512, 128, 2 * n)
    return np.ascontiguousarray(words), np.ascontiguousarray(byte.astype(np.uint8).reshape(k // 512, 16, n))


def unpack_weight(words, scales, fmt):
    g, _, n = scales.shape
    words = np.ascontiguousarray(words).reshape(g, 128, n, -1)
    if fmt == "e4m3":
        vals = words.view(ml_dtypes.float8_e4m3fn).astype(np.float64)
    else:
        nib = np.empty((g, 128, n, 4), np.uint8)
        nib[..., 0::2] = words & 0xF
        nib[..., 1::2] = words >> 4
        vals = E2M1[nib]
    vals = vals * np.repeat(np.exp2(scales.astype(np.float64) - 127.0), 8, axis=1)[..., None]
    return vals.transpose(0, 1, 3, 2).reshape(g * 512, n)


def gelu(v):
    return 0.5 * v * (1.0 + np.tanh(np.sqrt(2.0 / np.pi) * (v + 0.044715 * v**3)))


def striped8(idx):
    return np.concatenate([v.reshape(-1, 16).T for v in idx]).astype(np.uint16)


def unstriped8(offs):
    return np.stack([offs[16 * g:16 * g + 16].T.reshape(-1) for g in range(8)]).astype(np.int64)


def runs(v, idx8):
    k = np.arange(v.shape[0])
    return v[k[:, None], idx8[k % 512 // 64]]


T, S, T2, K, K2, H, N = 2048, 1024, 2048, 1024, 512, 1024, 512


def setup_inputs():
    n = np.random.standard_normal
    s = mx_kscale(K)[:, None]
    s2 = mx_kscale(K2)[:, None]
    u = mx_kscale(H)[:, None]
    tab_words, tab_scales = pack_weight(n((K, T)) * s, "e4m3")
    tab2_words, tab2_scales = pack_weight(n((K2, T)) * s2, "e4m3")
    w2_words, w2_scales = pack_weight(n((K2, H)) / np.sqrt(K2) / s2 * u.T, "e4m3")
    w4_words, w4_scales = pack_weight(n((H, N)) / np.sqrt(H) / u, "e2m1")
    return {
        "tab_words": tab_words, "tab_scales": tab_scales,
        "tab2_words": tab2_words, "tab2_scales": tab2_scales,
        "offs": striped8(np.stack([np.random.permutation(T)[:S] for _ in range(8)])),
        "offs2": striped(np.random.permutation(T)[:S]),
        "offs3": striped(np.random.permutation(T2)[:S]),
        "w1": (n((K, H)) / np.sqrt(K) / s * u.T).astype(np.float32),
        "b1": (0.7 * n(H) * u[:, 0]).astype(np.float32),
        "w2_words": w2_words, "w2_scales": w2_scales,
        "w3": (1.5 * n((K2, N)) / np.sqrt(K2) / s2).astype(np.float32),
        "w4_words": w4_words, "w4_scales": w4_scales,
        "wgo": np.exp(0.3 * n((128, S))).astype(np.float32),
        "page1": n((N, T2)).astype(np.float32),
    }


def reference(tab_words, tab_scales, tab2_words, tab2_scales, offs, offs2, offs3, w1, b1,
              w2_words, w2_scales, w3, w4_words, w4_scales, wgo, page1):
    v = runs(unpack_weight(tab_words, tab_scales, "e4m3"), unstriped8(offs))
    v2 = unpack_weight(tab2_words, tab2_scales, "e4m3")[:, unstriped(offs2)]
    cue = mxq(f64(w1), 0, "e4m3").T @ v
    shot = unpack_weight(w2_words, w2_scales, "e4m3").T @ v2
    h = np.abs(cue - shot + f64(b1)[:, None])
    q = mxq(f64(w3), 0, "e4m3").T @ v2
    e = unpack_weight(w4_words, w4_scales, "e2m1").T @ mxq(h, 0, "e4m3")
    y = e / (1.0 + np.abs(q))
    out = f64(page1).copy()
    out[:, unstriped(offs3)] = np.tile(f64(wgo), (N // 128, 1)) * y
    return out

@@ -1,0 +1,220 @@
+from contextlib import ExitStack
+
+import concourse.mybir as mybir
+
+T, S, T2, K, K2, H, N = 2048, 1024, 2048, 1024, 512, 1024, 512
+FLOPS = 2 * S * (K * H + K2 * H + K2 * N + H * N)
+
+F32 = mybir.dt.float32
+BF16 = mybir.dt.bfloat16
+I32 = mybir.dt.int32
+U32 = mybir.dt.uint32
+U16 = mybir.dt.uint16
+U8 = mybir.dt.uint8
+FP8X4 = mybir.dt.float8_e4m3fn_x4
+FP4X4 = mybir.dt.float4_e2m1fn_x4
+ACT = mybir.ActivationFunctionType
+MULT = mybir.AluOpType.mult
+
+P = 128
+PASS = 512
+CHUNKS = ((0, 256), (256, 256), (512, 512))
+
+
+def tile_list_cue_break_scores_kernel(
+    tc, tab_words, tab_scales, tab2_words, tab2_scales, offs, offs2, offs3, w1, b1,
+    w2_words, w2_scales, w3, w4_words, w4_scales, wgo, page1, out,
+):
+    nc = tc.nc
+    with ExitStack() as ctx:
+        keep = ctx.enter_context(tc.tile_pool(name="keep", bufs=1))
+        work = ctx.enter_context(tc.tile_pool(name="work", bufs=2))
+        psum_h = ctx.enter_context(tc.psum_pool(name="psum_h", bufs=4))
+        psum_q = ctx.enter_context(tc.psum_pool(name="psum_q", bufs=2))
+        psum_e = ctx.enter_context(tc.psum_pool(name="psum_e", bufs=2))
+
+        def held(name, shape, dtype):
+            return keep.tile(shape, dtype, name=name, align_bytes=64)
+
+        def words_of(dram):
+            return dram.rearrange("p c i -> p (c i)").bitcast(I32)
+
+        lists = held("lists", [P, S // 16], U16)
+        list2 = held("list2", [P, S // 16], U16)
+        list3 = held("list3", [P, S // 16], U16)
+        tab2_win = held("tab2_win", [P, T], I32)
+        tab2_swin = held("tab2_swin", [P, T], U8)
+        tab_swin = held("tab_swin", [P, T], U8)
+        w2_sraw = held("w2_sraw", [P, H], U8)
+        w4_planes = held("w4_planes", [P, 2, N], U8)
+        v_planes = held("v_planes", [P, S], U8)
+        for tile in (tab2_swin, tab_swin, w2_sraw):
+            nc.vector.memset(tile[:].bitcast(I32), 0)
+        nc.vector.memset(w4_planes[:].rearrange("p a c -> p (a c)").bitcast(I32), 0)
+
+        nc.sync.dma_start(list2[:], offs2)
+        nc.sync.dma_start(tab2_win[:], words_of(tab2_words[0]))
+        for d in range(4):
+            nc.sync.dma_start(tab2_swin[32 * d : 32 * d + 4, :].bitcast(I32), tab2_scales[0, 4 * d : 4 * d + 4, :].bitcast(I32))
+        nc.sync.dma_start(lists[:], offs)
+        w3_raw = held("w3_raw", [P, 4, N], F32)
+        nc.sync.dma_start(w3_raw[:], w3.rearrange("(p j) c -> p j c", j=4))
+        for a in range(2):
+            for r in range(2):
+                nc.sync.dma_start(tab_swin[4 * a + r : P : 16, :].bitcast(I32), tab_scales[a, r:16:2, :].bitcast(I32))
+        tab_win = [held(f"tab_win{a}", [P, T], I32) for a in range(2)]
+        for a in range(2):
+            nc.sync.dma_start(tab_win[a][:], words_of(tab_words[a]))
+        w2_raw = held("w2_raw", [P, H], I32)
+        nc.sync.dma_start(w2_raw[:], words_of(w2_words[0]))
+        for d in range(4):
+            nc.sync.dma_start(w2_sraw[32 * d : 32 * d + 4, :].bitcast(I32), w2_scales[0, 4 * d : 4 * d + 4, :].bitcast(I32))
+        bias = held("bias", [P, 2, 4], F32)
+        nc.sync.dma_start(bias[:], b1.rearrange("(b p t) -> p b t", b=2, t=4))
+        w1_raw = {}
+        for b in range(2):
+            for a in range(2):
+                w1_raw[a, b] = held(f"w1_raw{a}{b}", [P, 4, PASS], F32)
+                rows = w1[PASS * a : PASS * (a + 1), PASS * b : PASS * (b + 1)]
+                nc.sync.dma_start(w1_raw[a, b][:], rows.rearrange("(p j) c -> p j c", j=4))
+        w4_codes = held("w4_codes", [P, 2, 2 * N], U8)
+        nc.sync.dma_start(w4_codes[:].bitcast(I32), w4_words.rearrange("a p c -> p a c").bitcast(I32))
+        for d in range(4):
+            nc.sync.dma_start(
+                w4_planes[32 * d : 32 * d + 4, :, :].bitcast(I32),
+                w4_scales[:, 4 * d : 4 * d + 4, :].rearrange("a r c -> r a c").bitcast(I32),
+            )
+        gains = held("gains", [P, S], F32)
+        nc.sync.dma_start(gains[:], wgo)
+        nc.sync.dma_start(list3[:], offs3)
+        pages = [held(f"page{n}", [P, T2], F32) for n in range(4)]
+        for n in range(4):
+            nc.sync.dma_start(pages[n][:], page1[P * n : P * (n + 1), :])
+
+        v2_codes = held("v2_codes", [P, S], U32)
+        v2_plane = held("v2_plane", [P, S], U8)
+        nc.vector.tensor_copy(v2_codes[:], tab2_win[:].bitcast(U32).indirect(list2[:]))
+        nc.vector.tensor_copy(v2_plane[:], tab2_swin[:].indirect(list2[:]))
+
+        w3_bf = held("w3_bf", [P, N, 4], BF16)
+        nc.scalar.activation(
+            w3_bf[:].rearrange("p (c i) j -> p c j i", i=4), w3_raw[:].rearrange("p j (c i) -> p c j i", i=4), ACT.Copy
+        )
+        w3_codes = held("w3_codes", [P, N], U32)
+        w3_plane = held("w3_plane", [P, N], U8)
+        nc.vector.quantize_mx(w3_codes[:].bitcast(FP8X4), w3_plane[:], w3_bf[:].rearrange("p c j -> p (c j)"))
+
+        damp = {}
+
+        def damping(c):
+            j0, w = CHUNKS[c]
+            for n in range(4):
+                q = psum_q.tile([P, PASS], F32, name="q")
+                nc.tensor.matmul_mx(
+                    q[:, :w],
+                    lhsT=w3_codes[:, P * n : P * (n + 1)].bitcast(FP8X4), lhsT_scale=w3_plane[:, P * n : P * (n + 1)],
+                    rhs=v2_codes[:, j0 : j0 + w].bitcast(FP8X4), rhs_scale=v2_plane[:, j0 : j0 + w],
+                    start=True, stop=True,
+                )
+                size = work.tile([P, PASS], F32, name="size")
+                nc.scalar.activation(size[:, :w], q[:, :w], ACT.Abs)
+                root = work.tile([P, PASS], F32, name="root")
+                nc.scalar.activation(root[:, :w], size[:, :w], ACT.Abs_reciprocal_sqrt, bias=1.0)
+                damp[c, n] = held(f"damp{c}{n}", [P, w], F32)
+                nc.scalar.activation(damp[c, n][:], root[:, :w], ACT.Square)
+
+        damping(0)
+
+        v_picked = held("v_picked", [P, S], U8)
+        nc.vector.tensor_copy(v_picked[:], tab_swin[:].indirect(lists[:]))
+        nc.vector.tensor_copy(v_planes[:].bitcast(I32), v_picked[:].bitcast(I32))
+        for a in range(2):
+            for r in range(2):
+                nc.sync.dma_start(
+                    v_planes[4 * a + 2 + r : P : 32, :].bitcast(I32), v_picked[16 + 4 * a + r : P : 32, :].bitcast(I32)
+                )
+        v_codes = [held(f"v_codes{a}", [P, S], U32) for a in range(2)]
+        for a in range(2):
+            nc.vector.tensor_copy(v_codes[a][:], tab_win[a][:].bitcast(U32).indirect(lists[:]))
+
+        w2_codes = held("w2_codes", [P, H], I32)
+        w2_plane = held("w2_plane", [P, H], U8)
+        for dealt, raw in ((w2_codes, w2_raw), (w2_plane, w2_sraw)):
+            nc.vector.tensor_copy(
+                dealt[:].rearrange("p (b t m) -> p b m t", b=2, t=4), raw[:].rearrange("p (b m t) -> p b m t", b=2, t=4)
+            )
+
+        w1_codes, w1_plane = {}, {}
+
+        def quantise_w1(a, b):
+            w1_bf = work.tile([P, 4, P, 4], BF16, name="w1_bf", align_bytes=64)
+            dst = w1_bf[:].rearrange("p t m j -> p m j t")
+            src = w1_raw[a, b][:].rearrange("p j (m t) -> p m j t", t=4)
+            if b == 0:
+                nc.scalar.activation(dst, src, ACT.Copy, scale=-1.0)
+            else:
+                nc.vector.tensor_scalar_mul(dst, src, -1.0)
+            w1_codes[a, b] = held(f"w1_codes{a}{b}", [P, PASS], U32)
+            w1_plane[a, b] = held(f"w1_plane{a}{b}", [P, PASS], U8)
+            nc.vector.quantize_mx(
+                w1_codes[a, b][:].bitcast(FP8X4), w1_plane[a, b][:], w1_bf[:].rearrange("p t m j -> p (t m j)")
+            )
+
+        h_codes, h_plane = {}, {}
+
+        def first_stage(c, b):
+            j0, w = CHUNKS[c]
+            cols = slice(j0, j0 + w)
+            slots = work.tile([P, 4, w], BF16, name="slots", align_bytes=64)
+            for t in range(4):
+                acc = psum_h.tile([P, PASS], F32, name="acc")
+                m2 = slice(PASS * b + P * t, PASS * b + P * (t + 1))
+                m1 = slice(P * t, P * (t + 1))
+                nc.tensor.matmul_mx(
+                    acc[:, :w], lhsT=w2_codes[:, m2].bitcast(FP8X4), lhsT_scale=w2_plane[:, m2],
+                    rhs=v2_codes[:, cols].bitcast(FP8X4), rhs_scale=v2_plane[:, cols], start=True, stop=False,
+                )
+                for a in range(2):
+                    nc.tensor.matmul_mx(
+                        acc[:, :w], lhsT=w1_codes[a, b][:, m1].bitcast(FP8X4), lhsT_scale=w1_plane[a, b][:, m1],
+                        rhs=v_codes[a][:, cols].bitcast(FP8X4), rhs_scale=v_planes[4 * a : P, cols],
+                        start=False, stop=(a == 1),
+                    )
+                nc.scalar.activation(slots[:, t, :], acc[:, :w], ACT.Abs, bias=bias[:, b, t : t + 1], scale=-1.0)
+            woven = work.tile([P, w, 4], BF16, name="woven", align_bytes=64)
+            nc.scalar.copy(woven[:].rearrange("p (c i) t -> p c t i", i=4), slots[:].rearrange("p t (c i) -> p c t i", i=4))
+            h_codes[c, b] = held(f"h_codes{c}{b}", [P, w], U32)
+            h_plane[c, b] = held(f"h_plane{c}{b}", [P, w], U8)
+            nc.vector.quantize_mx(h_codes[c, b][:].bitcast(FP8X4), h_plane[c, b][:], woven[:].rearrange("p c t -> p (c t)"))
+
+        def second_stage(c, n):
+            j0, w = CHUNKS[c]
+            e = psum_e.tile([P, PASS], F32, name="e")
+            for b in range(2):
+                nc.tensor.matmul_mx(
+                    e[:, :w],
+                    lhsT=w4_codes[:, b, 2 * P * n : 2 * P * (n + 1)].bitcast(FP4X4),
+                    lhsT_scale=w4_planes[:, b, P * n : P * (n + 1)],
+                    rhs=h_codes[c, b][:].bitcast(FP8X4), rhs_scale=h_plane[c, b][:],
+                    start=(b == 0), stop=(b == 1),
+                )
+            y = work.tile([P, w], F32, name="y")
+            nc.vector.tensor_tensor(y[:], e[:, :w], damp[c, n][:], MULT)
+            places = list3[:, j0 // 16 : (j0 + w) // 16]
+            nc.vector.tensor_tensor(pages[n][:].indirect(places), y[:], gains[:, j0 : j0 + w], MULT)
+
+        for a in range(2):
+            quantise_w1(a, 0)
+        first_stage(0, 0)
+        for a in range(2):
+            quantise_w1(a, 1)
+        first_stage(0, 1)
+        for c in range(len(CHUNKS)):
+            if c + 1 < len(CHUNKS):
+                first_stage(c + 1, 0)
+                first_stage(c + 1, 1)
+                damping(c + 1)
+            for n in range(4):
+                second_stage(c, n)
+        for n in range(4):
+            nc.sync.dma_start(out[P * n : P * (n + 1), :], pages[n][:])

@@ -19,6 +19,7 @@ MULT = mybir.AluOpType.mult
 P = 128
 PASS = 512
 CHUNKS = ((0, 256), (256, 256), (512, 512))
+W = 256
 
 
 def tile_list_cue_break_scores_kernel(
@@ -33,8 +34,13 @@ def tile_list_cue_break_scores_kernel(
         psum_q = ctx.enter_context(tc.psum_pool(name="psum_q", bufs=2))
         psum_e = ctx.enter_context(tc.psum_pool(name="psum_e", bufs=2))
 
-        def held(name, shape, dtype):
-            return keep.tile(shape, dtype, name=name, align_bytes=64)
+        def held(name, shape, dtype, on=None):
+            return keep.tile(shape, dtype, name=name, tag=on or name, align_bytes=64)
+
+        def load_plane(tile, rows):
+            for r in range(4):
+                spread = rows[r:16:4, :].bitcast(I32).unsqueeze(1).broadcast_to([4, 8, rows.shape[1] // 4])
+                nc.sync.dma_start(tile[r:P:4, :].bitcast(I32), spread)
 
         def words_of(dram):
             return dram.rearrange("p c i -> p (c i)").bitcast(I32)
@@ -46,49 +52,67 @@ def tile_list_cue_break_scores_kernel(
         tab2_swin = held("tab2_swin", [P, T], U8)
         tab_swin = held("tab_swin", [P, T], U8)
         w2_sraw = held("w2_sraw", [P, H], U8)
-        w4_planes = held("w4_planes", [P, 2, N], U8)
         v_planes = held("v_planes", [P, S], U8)
-        for tile in (tab2_swin, tab_swin, w2_sraw):
-            nc.vector.memset(tile[:].bitcast(I32), 0)
-        nc.vector.memset(w4_planes[:].rearrange("p a c -> p (a c)").bitcast(I32), 0)
 
-        nc.sync.dma_start(list2[:], offs2)
-        nc.sync.dma_start(tab2_win[:], words_of(tab2_words[0]))
-        for d in range(4):
-            nc.sync.dma_start(tab2_swin[32 * d : 32 * d + 4, :].bitcast(I32), tab2_scales[0, 4 * d : 4 * d + 4, :].bitcast(I32))
         nc.sync.dma_start(lists[:], offs)
-        w3_raw = held("w3_raw", [P, 4, N], F32)
-        nc.sync.dma_start(w3_raw[:], w3.rearrange("(p j) c -> p j c", j=4))
         for a in range(2):
             for r in range(2):
-                nc.sync.dma_start(tab_swin[4 * a + r : P : 16, :].bitcast(I32), tab_scales[a, r:16:2, :].bitcast(I32))
+                spread = tab_scales[a, r:16:2, :].bitcast(I32).unsqueeze(1).broadcast_to([8, 4, T // 4])
+                nc.sync.dma_start(tab_swin[2 * a + r : P : 4, :].bitcast(I32), spread)
+        nc.sync.dma_start(list2[:], offs2)
+        nc.sync.dma_start(tab2_win[:], words_of(tab2_words[0]))
+        load_plane(tab2_swin, tab2_scales[0])
+        w3_raw = {}
+
+        def load_w3(u, on=None):
+            w3_raw[u] = held(f"w3_raw{u}", [P, 4, N // 2], F32, on=on)
+            nc.sync.dma_start(w3_raw[u][:], w3[:, N // 2 * u : N // 2 * (u + 1)].rearrange("(p j) c -> p j c", j=4))
+
+        load_w3(0)
         tab_win = [held(f"tab_win{a}", [P, T], I32) for a in range(2)]
         for a in range(2):
             nc.sync.dma_start(tab_win[a][:], words_of(tab_words[a]))
         w2_raw = held("w2_raw", [P, H], I32)
         nc.sync.dma_start(w2_raw[:], words_of(w2_words[0]))
+        nc.sync.dma_start(list3[:], offs3)
+        nc.gpsimd.memset(w2_sraw[:].bitcast(I32), 0)
         for d in range(4):
-            nc.sync.dma_start(w2_sraw[32 * d : 32 * d + 4, :].bitcast(I32), w2_scales[0, 4 * d : 4 * d + 4, :].bitcast(I32))
+            nc.gpsimd.dma_start(w2_sraw[32 * d : 32 * d + 4, :].bitcast(I32), w2_scales[0, 4 * d : 4 * d + 4, :].bitcast(I32))
         bias = held("bias", [P, 2, 4], F32)
-        nc.sync.dma_start(bias[:], b1.rearrange("(b p t) -> p b t", b=2, t=4))
-        w1_raw = {}
-        for b in range(2):
-            for a in range(2):
-                w1_raw[a, b] = held(f"w1_raw{a}{b}", [P, 4, PASS], F32)
-                rows = w1[PASS * a : PASS * (a + 1), PASS * b : PASS * (b + 1)]
-                nc.sync.dma_start(w1_raw[a, b][:], rows.rearrange("(p j) c -> p j c", j=4))
-        w4_codes = held("w4_codes", [P, 2, 2 * N], U8)
-        nc.sync.dma_start(w4_codes[:].bitcast(I32), w4_words.rearrange("a p c -> p a c").bitcast(I32))
+        nc.gpsimd.dma_start(bias[:], b1.rearrange("(b p t) -> p b t", b=2, t=4))
+        w4_planes = held("w4_planes", [P, 2, N], U8)
+        nc.gpsimd.memset(w4_planes[:].rearrange("p a c -> p (a c)").bitcast(I32), 0)
         for d in range(4):
-            nc.sync.dma_start(
+            nc.gpsimd.dma_start(
                 w4_planes[32 * d : 32 * d + 4, :, :].bitcast(I32),
                 w4_scales[:, 4 * d : 4 * d + 4, :].rearrange("a r c -> r a c").bitcast(I32),
             )
-        gains = held("gains", [P, S], F32)
-        nc.sync.dma_start(gains[:], wgo)
-        nc.sync.dma_start(list3[:], offs3)
-        pages = [held(f"page{n}", [P, T2], F32) for n in range(4)]
-        for n in range(4):
+
+        v_picked = held("v_picked", [P, S], U8)
+        nc.vector.tensor_copy(v_picked[:], tab_swin[:].indirect(lists[:]))
+        nc.vector.tensor_copy(v_planes[:].bitcast(I32), v_picked[:].bitcast(I32))
+        for a in range(2):
+            for r in range(4):
+                source = 16 * (r // 2) + 2 * a + r % 2
+                if source != 4 * a + r:
+                    nc.sync.dma_start(v_planes[4 * a + r : P : 32, :].bitcast(I32), v_picked[source:P:32, :].bitcast(I32))
+
+        w1_raw = {}
+
+        def load_w1(a, b, *on):
+            width = PASS // len(on)
+            w1_raw[a, b] = []
+            for u, tag in enumerate(on):
+                w1_raw[a, b].append(held(f"w1_raw{a}{b}{u}", [P, 4, width], F32, on=tag))
+                c0 = PASS * b + width * u
+                rows = w1[PASS * a : PASS * (a + 1), c0 : c0 + width]
+                nc.sync.dma_start(w1_raw[a, b][u][:], rows.rearrange("(p j) c -> p j c", j=4))
+
+        pages = []
+
+        def load_page(on):
+            n = len(pages)
+            pages.append(held(f"page{n}", [P, T2], F32, on=on))
             nc.sync.dma_start(pages[n][:], page1[P * n : P * (n + 1), :])
 
         v2_codes = held("v2_codes", [P, S], U32)
@@ -96,46 +120,48 @@ def tile_list_cue_break_scores_kernel(
         nc.vector.tensor_copy(v2_codes[:], tab2_win[:].bitcast(U32).indirect(list2[:]))
         nc.vector.tensor_copy(v2_plane[:], tab2_swin[:].indirect(list2[:]))
 
-        w3_bf = held("w3_bf", [P, N, 4], BF16)
-        nc.scalar.activation(
-            w3_bf[:].rearrange("p (c i) j -> p c j i", i=4), w3_raw[:].rearrange("p j (c i) -> p c j i", i=4), ACT.Copy
-        )
-        w3_codes = held("w3_codes", [P, N], U32)
-        w3_plane = held("w3_plane", [P, N], U8)
-        nc.vector.quantize_mx(w3_codes[:].bitcast(FP8X4), w3_plane[:], w3_bf[:].rearrange("p c j -> p (c j)"))
+        w3_codes, w3_plane = {}, {}
 
-        damp = {}
+        def quantise_w3(u):
+            w3_bf = held(f"w3_bf{u}", [P, N // 2, 4], BF16)
+            cast = nc.scalar.copy if u == 0 else nc.vector.tensor_copy
+            cast(w3_bf[:].rearrange("p (c i) j -> p c j i", i=4), w3_raw[u][:].rearrange("p j (c i) -> p c j i", i=4))
+            w3_codes[u] = held(f"w3_codes{u}", [P, N // 2], U32)
+            w3_plane[u] = held(f"w3_plane{u}", [P, N // 2], U8)
+            nc.vector.quantize_mx(w3_codes[u][:].bitcast(FP8X4), w3_plane[u][:], w3_bf[:].rearrange("p c j -> p (c j)"))
 
-        def damping(c):
-            j0, w = CHUNKS[c]
-            for n in range(4):
-                q = psum_q.tile([P, PASS], F32, name="q")
-                nc.tensor.matmul_mx(
-                    q[:, :w],
-                    lhsT=w3_codes[:, P * n : P * (n + 1)].bitcast(FP8X4), lhsT_scale=w3_plane[:, P * n : P * (n + 1)],
-                    rhs=v2_codes[:, j0 : j0 + w].bitcast(FP8X4), rhs_scale=v2_plane[:, j0 : j0 + w],
-                    start=True, stop=True,
-                )
+        quantise_w3(0)
+        load_w1(0, 0, "tab_swin")
+        load_w1(1, 0, "tab2_win")
+        load_w1(0, 1, "tab2_swin")
+
+        damp = held("damp", [P, 4, S], F32)
+
+        def damping(n, half, after=None):
+            cols = slice(PASS * half, PASS * (half + 1))
+            m = slice(P * (n % 2), P * (n % 2 + 1))
+            q = psum_q.tile([P, PASS], F32, name="q")
+            nc.tensor.matmul_mx(
+                q[:], lhsT=w3_codes[n // 2][:, m].bitcast(FP8X4), lhsT_scale=w3_plane[n // 2][:, m],
+                rhs=v2_codes[:, cols].bitcast(FP8X4), rhs_scale=v2_plane[:, cols], start=True, stop=True,
+            )
+            if after is None:
                 size = work.tile([P, PASS], F32, name="size")
-                nc.scalar.activation(size[:, :w], q[:, :w], ACT.Abs)
-                root = work.tile([P, PASS], F32, name="root")
-                nc.scalar.activation(root[:, :w], size[:, :w], ACT.Abs_reciprocal_sqrt, bias=1.0)
-                damp[c, n] = held(f"damp{c}{n}", [P, w], F32)
-                nc.scalar.activation(damp[c, n][:], root[:, :w], ACT.Square)
+            else:
+                size = held("size_held", [P, PASS], F32, on=after)
+            nc.scalar.activation(size[:], q[:], ACT.Abs)
+            root = work.tile([P, PASS], F32, name="root")
+            nc.scalar.activation(root[:], size[:], ACT.Abs_reciprocal_sqrt, bias=1.0)
+            nc.scalar.activation(damp[:, n, cols], root[:], ACT.Square)
 
-        damping(0)
+        damping(0, 0)
+        damping(1, 0)
 
-        v_picked = held("v_picked", [P, S], U8)
-        nc.vector.tensor_copy(v_picked[:], tab_swin[:].indirect(lists[:]))
-        nc.vector.tensor_copy(v_planes[:].bitcast(I32), v_picked[:].bitcast(I32))
-        for a in range(2):
-            for r in range(2):
-                nc.sync.dma_start(
-                    v_planes[4 * a + 2 + r : P : 32, :].bitcast(I32), v_picked[16 + 4 * a + r : P : 32, :].bitcast(I32)
-                )
         v_codes = [held(f"v_codes{a}", [P, S], U32) for a in range(2)]
         for a in range(2):
             nc.vector.tensor_copy(v_codes[a][:], tab_win[a][:].bitcast(U32).indirect(lists[:]))
+
+        load_w1(1, 1, "tab_win0", "tab_win1")
 
         w2_codes = held("w2_codes", [P, H], I32)
         w2_plane = held("w2_plane", [P, H], U8)
@@ -144,77 +170,134 @@ def tile_list_cue_break_scores_kernel(
                 dealt[:].rearrange("p (b t m) -> p b m t", b=2, t=4), raw[:].rearrange("p (b m t) -> p b m t", b=2, t=4)
             )
 
+        w4_codes = held("w4_codes", [P, 2, 2 * N], U8, on="w2_raw")
+        nc.sync.dma_start(w4_codes[:].bitcast(I32), w4_words.rearrange("a p c -> p a c").bitcast(I32))
+
         w1_codes, w1_plane = {}, {}
 
         def quantise_w1(a, b):
-            w1_bf = work.tile([P, 4, P, 4], BF16, name="w1_bf", align_bytes=64)
+            w1_bf = held(f"w1_bf{a}{b}", [P, 4, P, 4], BF16)
             dst = w1_bf[:].rearrange("p t m j -> p m j t")
-            src = w1_raw[a, b][:].rearrange("p j (m t) -> p m j t", t=4)
-            if b == 0:
-                nc.scalar.activation(dst, src, ACT.Copy, scale=-1.0)
-            else:
-                nc.vector.tensor_scalar_mul(dst, src, -1.0)
+            parts = len(w1_raw[a, b])
+            for u in range(parts):
+                m = slice(P // parts * u, P // parts * (u + 1))
+                src = w1_raw[a, b][u][:].rearrange("p j (m t) -> p m j t", t=4)
+                if a != b:
+                    nc.scalar.activation(dst[:, m], src, ACT.Copy, scale=-1.0)
+                else:
+                    nc.vector.tensor_scalar_mul(dst[:, m], src, -1.0)
             w1_codes[a, b] = held(f"w1_codes{a}{b}", [P, PASS], U32)
             w1_plane[a, b] = held(f"w1_plane{a}{b}", [P, PASS], U8)
-            nc.vector.quantize_mx(
-                w1_codes[a, b][:].bitcast(FP8X4), w1_plane[a, b][:], w1_bf[:].rearrange("p t m j -> p (t m j)")
-            )
+            flat = w1_bf[:].rearrange("p t m j -> p (t m j)")
+            for u in range(parts):
+                c0, c1 = PASS // parts * u, PASS // parts * (u + 1)
+                nc.vector.quantize_mx(
+                    w1_codes[a, b][:, c0:c1].bitcast(FP8X4), w1_plane[a, b][:, c0:c1], flat[:, 4 * c0 : 4 * c1]
+                )
 
-        h_codes, h_plane = {}, {}
+        h_codes, h_plane = [], []
 
         def first_stage(c, b):
-            j0, w = CHUNKS[c]
-            cols = slice(j0, j0 + w)
-            slots = work.tile([P, 4, w], BF16, name="slots", align_bytes=64)
-            for t in range(4):
-                acc = psum_h.tile([P, PASS], F32, name="acc")
-                m2 = slice(PASS * b + P * t, PASS * b + P * (t + 1))
-                m1 = slice(P * t, P * (t + 1))
-                nc.tensor.matmul_mx(
-                    acc[:, :w], lhsT=w2_codes[:, m2].bitcast(FP8X4), lhsT_scale=w2_plane[:, m2],
-                    rhs=v2_codes[:, cols].bitcast(FP8X4), rhs_scale=v2_plane[:, cols], start=True, stop=False,
-                )
-                for a in range(2):
+            cols = slice(W * c, W * (c + 1))
+            slots = held(f"slots{c}{b}", [P, 4, W], BF16)
+            for pair in range(2):
+                acc = psum_h.tile([P, 2, W], F32, name="acc")
+                for i in range(2):
+                    m2 = slice(PASS * b + P * (2 * pair + i), PASS * b + P * (2 * pair + i + 1))
                     nc.tensor.matmul_mx(
-                        acc[:, :w], lhsT=w1_codes[a, b][:, m1].bitcast(FP8X4), lhsT_scale=w1_plane[a, b][:, m1],
-                        rhs=v_codes[a][:, cols].bitcast(FP8X4), rhs_scale=v_planes[4 * a : P, cols],
-                        start=False, stop=(a == 1),
+                        acc[:, i, :], lhsT=w2_codes[:, m2].bitcast(FP8X4), lhsT_scale=w2_plane[:, m2],
+                        rhs=v2_codes[:, cols].bitcast(FP8X4), rhs_scale=v2_plane[:, cols], start=(i == 0), stop=False,
                     )
-                nc.scalar.activation(slots[:, t, :], acc[:, :w], ACT.Abs, bias=bias[:, b, t : t + 1], scale=-1.0)
-            woven = work.tile([P, w, 4], BF16, name="woven", align_bytes=64)
-            nc.scalar.copy(woven[:].rearrange("p (c i) t -> p c t i", i=4), slots[:].rearrange("p t (c i) -> p c t i", i=4))
-            h_codes[c, b] = held(f"h_codes{c}{b}", [P, w], U32)
-            h_plane[c, b] = held(f"h_plane{c}{b}", [P, w], U8)
-            nc.vector.quantize_mx(h_codes[c, b][:].bitcast(FP8X4), h_plane[c, b][:], woven[:].rearrange("p c t -> p (c t)"))
+                for a in range(2):
+                    for i in range(2):
+                        m1 = slice(P * (2 * pair + i), P * (2 * pair + i + 1))
+                        nc.tensor.matmul_mx(
+                            acc[:, i, :], lhsT=w1_codes[a, b][:, m1].bitcast(FP8X4), lhsT_scale=w1_plane[a, b][:, m1],
+                            rhs=v_codes[a][:, cols].bitcast(FP8X4), rhs_scale=v_planes[4 * a : P, cols],
+                            start=False, stop=(a == 1 and i == 1),
+                        )
+                for i in range(2):
+                    t = 2 * pair + i
+                    nc.scalar.activation(slots[:, t, :], acc[:, i, :], ACT.Abs, bias=bias[:, b, t : t + 1], scale=-1.0)
+            woven = work.tile([P, W, 4], BF16, name="woven", bufs=4, align_bytes=64)
+            weave = nc.vector.tensor_copy if (c, b) == (0, 1) else nc.scalar.copy
+            weave(woven[:].rearrange("p (c i) t -> p c t i", i=4), slots[:].rearrange("p t (c i) -> p c t i", i=4))
+            return woven
+
+        def quantise_h(c, b, woven):
+            cols = slice(W * c, W * (c + 1))
+            nc.vector.quantize_mx(h_codes[b][:, cols].bitcast(FP8X4), h_plane[b][:, cols], woven[:].rearrange("p c t -> p (c t)"))
+
+        e_banks, ys = {}, {}
 
         def second_stage(c, n):
             j0, w = CHUNKS[c]
             e = psum_e.tile([P, PASS], F32, name="e")
-            for b in range(2):
-                nc.tensor.matmul_mx(
-                    e[:, :w],
-                    lhsT=w4_codes[:, b, 2 * P * n : 2 * P * (n + 1)].bitcast(FP4X4),
-                    lhsT_scale=w4_planes[:, b, P * n : P * (n + 1)],
-                    rhs=h_codes[c, b][:].bitcast(FP8X4), rhs_scale=h_plane[c, b][:],
-                    start=(b == 0), stop=(b == 1),
-                )
-            y = work.tile([P, w], F32, name="y")
-            nc.vector.tensor_tensor(y[:], e[:, :w], damp[c, n][:], MULT)
-            places = list3[:, j0 // 16 : (j0 + w) // 16]
-            nc.vector.tensor_tensor(pages[n][:].indirect(places), y[:], gains[:, j0 : j0 + w], MULT)
+            for i in range(PASS // w):
+                e_banks[c, n + i] = e[:, w * i : w * (i + 1)]
+                for b in (1, 0):
+                    nc.tensor.matmul_mx(
+                        e_banks[c, n + i],
+                        lhsT=w4_codes[:, b, 2 * P * (n + i) : 2 * P * (n + i + 1)].bitcast(FP4X4),
+                        lhsT_scale=w4_planes[:, b, P * (n + i) : P * (n + i + 1)],
+                        rhs=h_codes[b][:, j0 : j0 + w].bitcast(FP8X4), rhs_scale=h_plane[b][:, j0 : j0 + w],
+                        start=(b == 1), stop=(b == 0),
+                    )
 
-        for a in range(2):
-            quantise_w1(a, 0)
-        first_stage(0, 0)
-        for a in range(2):
-            quantise_w1(a, 1)
-        first_stage(0, 1)
-        for c in range(len(CHUNKS)):
-            if c + 1 < len(CHUNKS):
-                first_stage(c + 1, 0)
-                first_stage(c + 1, 1)
-                damping(c + 1)
-            for n in range(4):
+        def damped(c, n, on=None):
+            j0, w = CHUNKS[c]
+            if n % (PASS // w) == 0:
                 second_stage(c, n)
+            if on is None:
+                ys[c, n] = work.tile([P, w], F32, name="y", bufs=3)
+            else:
+                ys[c, n] = held("y_held", [P, w], F32, on=on)
+            nc.vector.tensor_tensor(ys[c, n][:], e_banks[c, n], damp[:, n, j0 : j0 + w], MULT)
+
+        def place(c, n):
+            j0, w = CHUNKS[c]
+            places = list3[:, j0 // 16 : (j0 + w) // 16]
+            nc.vector.tensor_tensor(pages[n][:].indirect(places), ys[c, n][:], gains[:, j0 : j0 + w], MULT)
+
+        quantise_w1(0, 0)
+        load_w3(1, on="tab_swin")
+        load_page(on="w2_sraw")
+        gains = held("gains", [P, S], F32, on="w1_bf00")
+        nc.sync.dma_start(gains[:], wgo)
+        quantise_w1(1, 0)
+        load_page(on="tab2_win")
+        quantise_w1(0, 1)
+        load_page(on="tab2_swin")
+        quantise_w1(1, 1)
+        load_page(on="tab_win0")
+        for b in range(2):
+            h_codes.append(held(f"h_codes{b}", [P, S], U32, on="w1_bf11" if b == 0 else None))
+            h_plane.append(held(f"h_plane{b}", [P, S], U8))
+        quantise_h(0, 0, first_stage(0, 0))
+        quantise_w3(1)
+        quantise_h(0, 1, first_stage(0, 1))
+        damping(2, 0, after="slots01")
+        damping(3, 0)
+        ahead = {0: (1,), 1: (2, 3), 2: ()}
+        for c in range(len(CHUNKS)):
+            damped(c, 0)
+            for n in range(3):
+                if n < 2:
+                    damped(c, n + 1)
+                place(c, n)
+            if ahead[c]:
+                last = ahead[c][-1]
+                for h in ahead[c]:
+                    quantise_h(h, 0, first_stage(h, 0))
+                    woven = first_stage(h, 1)
+                    if h == last:
+                        damped(c, 3, on=f"slots{last}1")
+                    quantise_h(h, 1, woven)
+            else:
+                damped(c, 3)
+            place(c, 3)
+            if c == 1:
+                for n in range(4):
+                    damping(n, 1)
         for n in range(4):
             nc.sync.dma_start(out[P * n : P * (n + 1), :], pages[n][:])

@@ -20,6 +20,8 @@ P = 128
 PASS = 512
 CHUNKS = ((0, 256), (256, 256), (512, 512))
 W = 256
+VW = ((0, 0), (0, 1), (1, 0))
+HB, QB, EB = 4, 2, 2
 
 
 def tile_list_cue_break_scores_kernel(
@@ -30,9 +32,9 @@ def tile_list_cue_break_scores_kernel(
     with ExitStack() as ctx:
         keep = ctx.enter_context(tc.tile_pool(name="keep", bufs=1))
         work = ctx.enter_context(tc.tile_pool(name="work", bufs=2))
-        psum_h = ctx.enter_context(tc.psum_pool(name="psum_h", bufs=4))
-        psum_q = ctx.enter_context(tc.psum_pool(name="psum_q", bufs=2))
-        psum_e = ctx.enter_context(tc.psum_pool(name="psum_e", bufs=2))
+        psum_h = ctx.enter_context(tc.psum_pool(name="psum_h", bufs=HB))
+        psum_q = ctx.enter_context(tc.psum_pool(name="psum_q", bufs=QB))
+        psum_e = ctx.enter_context(tc.psum_pool(name="psum_e", bufs=EB))
 
         def held(name, shape, dtype, on=None):
             return keep.tile(shape, dtype, name=name, tag=on or name, align_bytes=64)
@@ -72,9 +74,6 @@ def tile_list_cue_break_scores_kernel(
         tab_win = [held(f"tab_win{a}", [P, T], I32) for a in range(2)]
         for a in range(2):
             nc.sync.dma_start(tab_win[a][:], words_of(tab_words[a]))
-        w2_raw = held("w2_raw", [P, H], I32)
-        nc.sync.dma_start(w2_raw[:], words_of(w2_words[0]))
-        nc.sync.dma_start(list3[:], offs3)
         nc.gpsimd.memset(w2_sraw[:].bitcast(I32), 0)
         for d in range(4):
             nc.gpsimd.dma_start(w2_sraw[32 * d : 32 * d + 4, :].bitcast(I32), w2_scales[0, 4 * d : 4 * d + 4, :].bitcast(I32))
@@ -91,11 +90,12 @@ def tile_list_cue_break_scores_kernel(
         v_picked = held("v_picked", [P, S], U8)
         nc.vector.tensor_copy(v_picked[:], tab_swin[:].indirect(lists[:]))
         nc.vector.tensor_copy(v_planes[:].bitcast(I32), v_picked[:].bitcast(I32))
-        for a in range(2):
-            for r in range(4):
+
+        def move_rows(rows):
+            for row in rows:
+                a, r = divmod(row, 4)
                 source = 16 * (r // 2) + 2 * a + r % 2
-                if source != 4 * a + r:
-                    nc.sync.dma_start(v_planes[4 * a + r : P : 32, :].bitcast(I32), v_picked[source:P:32, :].bitcast(I32))
+                nc.sync.dma_start(v_planes[row:P:32, :].bitcast(I32), v_picked[source:P:32, :].bitcast(I32))
 
         w1_raw = {}
 
@@ -107,6 +107,12 @@ def tile_list_cue_break_scores_kernel(
                 c0 = PASS * b + width * u
                 rows = w1[PASS * a : PASS * (a + 1), c0 : c0 + width]
                 nc.sync.dma_start(w1_raw[a, b][u][:], rows.rearrange("(p j) c -> p j c", j=4))
+
+        move_rows((2, 3, 4))
+        w2_raw = held("w2_raw", [P, H], I32)
+        nc.sync.dma_start(w2_raw[:], words_of(w2_words[0]))
+        load_w1(0, 0, "tab_swin")
+        move_rows((5, 6, 7))
 
         pages = []
 
@@ -131,8 +137,8 @@ def tile_list_cue_break_scores_kernel(
             nc.vector.quantize_mx(w3_codes[u][:].bitcast(FP8X4), w3_plane[u][:], w3_bf[:].rearrange("p c j -> p (c j)"))
 
         quantise_w3(0)
-        load_w1(0, 0, "tab_swin")
         load_w1(1, 0, "tab2_win")
+        nc.sync.dma_start(list3[:], offs3)
         load_w1(0, 1, "tab2_swin")
 
         damp = held("damp", [P, 4, S], F32)
@@ -156,15 +162,17 @@ def tile_list_cue_break_scores_kernel(
 
         damping(0, 0)
         damping(1, 0)
+        damping(0, 1)
+        damping(1, 1)
 
-        v_codes = [held(f"v_codes{a}", [P, S], U32) for a in range(2)]
+        v_codes = [held(f"v_codes{a}", [P, S], U32, on="w3_bf0" if a == 0 else None) for a in range(2)]
         for a in range(2):
             nc.vector.tensor_copy(v_codes[a][:], tab_win[a][:].bitcast(U32).indirect(lists[:]))
 
         load_w1(1, 1, "tab_win0", "tab_win1")
 
         w2_codes = held("w2_codes", [P, H], I32)
-        w2_plane = held("w2_plane", [P, H], U8)
+        w2_plane = held("w2_plane", [P, H], U8, on="v_picked")
         for dealt, raw in ((w2_codes, w2_raw), (w2_plane, w2_sraw)):
             nc.vector.tensor_copy(
                 dealt[:].rearrange("p (b t m) -> p b m t", b=2, t=4), raw[:].rearrange("p (b m t) -> p b m t", b=2, t=4)
@@ -182,7 +190,7 @@ def tile_list_cue_break_scores_kernel(
             for u in range(parts):
                 m = slice(P // parts * u, P // parts * (u + 1))
                 src = w1_raw[a, b][u][:].rearrange("p j (m t) -> p m j t", t=4)
-                if a != b:
+                if (a, b) == (0, 1):
                     nc.scalar.activation(dst[:, m], src, ACT.Copy, scale=-1.0)
                 else:
                     nc.vector.tensor_scalar_mul(dst[:, m], src, -1.0)
@@ -220,7 +228,7 @@ def tile_list_cue_break_scores_kernel(
                     t = 2 * pair + i
                     nc.scalar.activation(slots[:, t, :], acc[:, i, :], ACT.Abs, bias=bias[:, b, t : t + 1], scale=-1.0)
             woven = work.tile([P, W, 4], BF16, name="woven", bufs=4, align_bytes=64)
-            weave = nc.vector.tensor_copy if (c, b) == (0, 1) else nc.scalar.copy
+            weave = nc.vector.tensor_copy if (c, b) in VW else nc.scalar.copy
             weave(woven[:].rearrange("p (c i) t -> p c t i", i=4), slots[:].rearrange("p t (c i) -> p c t i", i=4))
             return woven
 
@@ -235,13 +243,14 @@ def tile_list_cue_break_scores_kernel(
             e = psum_e.tile([P, PASS], F32, name="e")
             for i in range(PASS // w):
                 e_banks[c, n + i] = e[:, w * i : w * (i + 1)]
-                for b in (1, 0):
+                order = (0, 1) if c == 0 else (1, 0)
+                for b in order:
                     nc.tensor.matmul_mx(
                         e_banks[c, n + i],
                         lhsT=w4_codes[:, b, 2 * P * (n + i) : 2 * P * (n + i + 1)].bitcast(FP4X4),
                         lhsT_scale=w4_planes[:, b, P * (n + i) : P * (n + i + 1)],
                         rhs=h_codes[b][:, j0 : j0 + w].bitcast(FP8X4), rhs_scale=h_plane[b][:, j0 : j0 + w],
-                        start=(b == 1), stop=(b == 0),
+                        start=(b == order[0]), stop=(b == order[1]),
                     )
 
         def damped(c, n, on=None):
@@ -297,7 +306,7 @@ def tile_list_cue_break_scores_kernel(
                 damped(c, 3)
             place(c, 3)
             if c == 1:
-                for n in range(4):
+                for n in (2, 3):
                     damping(n, 1)
         for n in range(4):
             nc.sync.dma_start(out[P * n : P * (n + 1), :], pages[n][:])

@@ -20,8 +20,10 @@ P = 128
 PASS = 512
 CHUNKS = ((0, 256), (256, 256), (512, 512))
 W = 256
-VW = ((0, 0), (0, 1), (1, 0))
-HB, QB, EB = 4, 2, 2
+SC = ((0, 0, 0),)
+W3S = (0,)
+EARLY = 2
+VW = ((0, 1), (1, 0))
 
 
 def tile_list_cue_break_scores_kernel(
@@ -32,17 +34,10 @@ def tile_list_cue_break_scores_kernel(
     with ExitStack() as ctx:
         keep = ctx.enter_context(tc.tile_pool(name="keep", bufs=1))
         work = ctx.enter_context(tc.tile_pool(name="work", bufs=2))
-        psum_h = ctx.enter_context(tc.psum_pool(name="psum_h", bufs=HB))
-        psum_q = ctx.enter_context(tc.psum_pool(name="psum_q", bufs=QB))
-        psum_e = ctx.enter_context(tc.psum_pool(name="psum_e", bufs=EB))
+        psum = ctx.enter_context(tc.psum_pool(name="psum", bufs=2))
 
         def held(name, shape, dtype, on=None):
             return keep.tile(shape, dtype, name=name, tag=on or name, align_bytes=64)
-
-        def load_plane(tile, rows):
-            for r in range(4):
-                spread = rows[r:16:4, :].bitcast(I32).unsqueeze(1).broadcast_to([4, 8, rows.shape[1] // 4])
-                nc.sync.dma_start(tile[r:P:4, :].bitcast(I32), spread)
 
         def words_of(dram):
             return dram.rearrange("p c i -> p (c i)").bitcast(I32)
@@ -56,14 +51,17 @@ def tile_list_cue_break_scores_kernel(
         w2_sraw = held("w2_sraw", [P, H], U8)
         v_planes = held("v_planes", [P, S], U8)
 
+        nc.vector.memset(tab_swin[:].bitcast(I32), 0)
+        nc.vector.memset(tab2_swin[:].bitcast(I32), 0)
         nc.sync.dma_start(lists[:], offs)
+        nc.sync.dma_start(list2[:], offs2)
+        nc.sync.dma_start(list3[:], offs3)
         for a in range(2):
             for r in range(2):
-                spread = tab_scales[a, r:16:2, :].bitcast(I32).unsqueeze(1).broadcast_to([8, 4, T // 4])
-                nc.sync.dma_start(tab_swin[2 * a + r : P : 4, :].bitcast(I32), spread)
-        nc.sync.dma_start(list2[:], offs2)
+                nc.sync.dma_start(tab_swin[4 * a + r : P : 16, :].bitcast(I32), tab_scales[a, r:16:2, :].bitcast(I32))
         nc.sync.dma_start(tab2_win[:], words_of(tab2_words[0]))
-        load_plane(tab2_swin, tab2_scales[0])
+        for r in range(4):
+            nc.sync.dma_start(tab2_swin[r:P:32, :].bitcast(I32), tab2_scales[0, r:16:4, :].bitcast(I32))
         w3_raw = {}
 
         def load_w3(u, on=None):
@@ -71,31 +69,17 @@ def tile_list_cue_break_scores_kernel(
             nc.sync.dma_start(w3_raw[u][:], w3[:, N // 2 * u : N // 2 * (u + 1)].rearrange("(p j) c -> p j c", j=4))
 
         load_w3(0)
-        tab_win = [held(f"tab_win{a}", [P, T], I32) for a in range(2)]
-        for a in range(2):
-            nc.sync.dma_start(tab_win[a][:], words_of(tab_words[a]))
         nc.gpsimd.memset(w2_sraw[:].bitcast(I32), 0)
-        for d in range(4):
-            nc.gpsimd.dma_start(w2_sraw[32 * d : 32 * d + 4, :].bitcast(I32), w2_scales[0, 4 * d : 4 * d + 4, :].bitcast(I32))
+        for r in range(4):
+            nc.gpsimd.dma_start(w2_sraw[r:P:32, :].bitcast(I32), w2_scales[0, r:16:4, :].bitcast(I32))
         bias = held("bias", [P, 2, 4], F32)
         nc.gpsimd.dma_start(bias[:], b1.rearrange("(b p t) -> p b t", b=2, t=4))
         w4_planes = held("w4_planes", [P, 2, N], U8)
         nc.gpsimd.memset(w4_planes[:].rearrange("p a c -> p (a c)").bitcast(I32), 0)
-        for d in range(4):
+        for r in range(4):
             nc.gpsimd.dma_start(
-                w4_planes[32 * d : 32 * d + 4, :, :].bitcast(I32),
-                w4_scales[:, 4 * d : 4 * d + 4, :].rearrange("a r c -> r a c").bitcast(I32),
+                w4_planes[r:P:32, :, :].bitcast(I32), w4_scales[:, r:16:4, :].rearrange("a d c -> d a c").bitcast(I32)
             )
-
-        v_picked = held("v_picked", [P, S], U8)
-        nc.vector.tensor_copy(v_picked[:], tab_swin[:].indirect(lists[:]))
-        nc.vector.tensor_copy(v_planes[:].bitcast(I32), v_picked[:].bitcast(I32))
-
-        def move_rows(rows):
-            for row in rows:
-                a, r = divmod(row, 4)
-                source = 16 * (r // 2) + 2 * a + r % 2
-                nc.sync.dma_start(v_planes[row:P:32, :].bitcast(I32), v_picked[source:P:32, :].bitcast(I32))
 
         w1_raw = {}
 
@@ -108,11 +92,26 @@ def tile_list_cue_break_scores_kernel(
                 rows = w1[PASS * a : PASS * (a + 1), c0 : c0 + width]
                 nc.sync.dma_start(w1_raw[a, b][u][:], rows.rearrange("(p j) c -> p j c", j=4))
 
-        move_rows((2, 3, 4))
+        load_w1(0, 0, None)
+        tab_win = [held(f"tab_win{a}", [P, T], I32) for a in range(2)]
+        nc.sync.dma_start(tab_win[0][:], words_of(tab_words[0]))
+        nc.sync.dma_start(tab_win[1][:], words_of(tab_words[1]))
+
+        v_picked = held("v_picked", [P, S], U8)
+        nc.vector.tensor_copy(v_picked[:], tab_swin[:].indirect(lists[:]))
+        nc.vector.tensor_copy(v_planes[:].bitcast(I32), v_picked[:].bitcast(I32))
+
+        def move_rows(a):
+            for r in range(2):
+                nc.sync.dma_start(
+                    v_planes[4 * a + 2 + r : P : 32, :].bitcast(I32), v_picked[16 + 4 * a + r : P : 32, :].bitcast(I32)
+                )
+
+        move_rows(0)
         w2_raw = held("w2_raw", [P, H], I32)
         nc.sync.dma_start(w2_raw[:], words_of(w2_words[0]))
-        load_w1(0, 0, "tab_swin")
-        move_rows((5, 6, 7))
+        load_w1(1, 0, "tab_swin")
+        move_rows(1)
 
         pages = []
 
@@ -130,23 +129,21 @@ def tile_list_cue_break_scores_kernel(
 
         def quantise_w3(u):
             w3_bf = held(f"w3_bf{u}", [P, N // 2, 4], BF16)
-            cast = nc.scalar.copy if u == 0 else nc.vector.tensor_copy
+            cast = nc.scalar.copy if u in W3S else nc.vector.tensor_copy
             cast(w3_bf[:].rearrange("p (c i) j -> p c j i", i=4), w3_raw[u][:].rearrange("p j (c i) -> p c j i", i=4))
             w3_codes[u] = held(f"w3_codes{u}", [P, N // 2], U32)
             w3_plane[u] = held(f"w3_plane{u}", [P, N // 2], U8)
             nc.vector.quantize_mx(w3_codes[u][:].bitcast(FP8X4), w3_plane[u][:], w3_bf[:].rearrange("p c j -> p (c j)"))
 
         quantise_w3(0)
-        load_w1(1, 0, "tab2_win")
-        nc.sync.dma_start(list3[:], offs3)
-        load_w1(0, 1, "tab2_swin")
+        load_w1(0, 1, "tab2_win")
 
         damp = held("damp", [P, 4, S], F32)
 
-        def damping(n, half, after=None):
+        def damping(n, half, after=None, banks="q"):
             cols = slice(PASS * half, PASS * (half + 1))
             m = slice(P * (n % 2), P * (n % 2 + 1))
-            q = psum_q.tile([P, PASS], F32, name="q")
+            q = psum.tile([P, PASS], F32, name="q", tag=banks)
             nc.tensor.matmul_mx(
                 q[:], lhsT=w3_codes[n // 2][:, m].bitcast(FP8X4), lhsT_scale=w3_plane[n // 2][:, m],
                 rhs=v2_codes[:, cols].bitcast(FP8X4), rhs_scale=v2_plane[:, cols], start=True, stop=True,
@@ -160,16 +157,43 @@ def tile_list_cue_break_scores_kernel(
             nc.scalar.activation(root[:], size[:], ACT.Abs_reciprocal_sqrt, bias=1.0)
             nc.scalar.activation(damp[:, n, cols], root[:], ACT.Square)
 
-        damping(0, 0)
+        w1_codes, w1_plane = {}, {}
+
+        def cast_w1(a, b):
+            w1_bf = held(f"w1_bf{a}{b}", [P, 4, P, 4], BF16)
+            dst = w1_bf[:].rearrange("p t m j -> p m j t")
+            parts = len(w1_raw[a, b])
+            for u in range(parts):
+                m = slice(P // parts * u, P // parts * (u + 1))
+                src = w1_raw[a, b][u][:].rearrange("p j (m t) -> p m j t", t=4)
+                if (a, b, u) in SC:
+                    nc.scalar.activation(dst[:, m], src, ACT.Copy, scale=-1.0)
+                else:
+                    nc.vector.tensor_scalar_mul(dst[:, m], src, -1.0)
+            return w1_bf
+
+        def quantise_w1(a, b, w1_bf, on=None):
+            parts = len(w1_raw[a, b])
+            w1_codes[a, b] = held(f"w1_codes{a}{b}", [P, PASS], U32, on=on)
+            w1_plane[a, b] = held(f"w1_plane{a}{b}", [P, PASS], U8)
+            flat = w1_bf[:].rearrange("p t m j -> p (t m j)")
+            for u in range(parts):
+                c0, c1 = PASS // parts * u, PASS // parts * (u + 1)
+                nc.vector.quantize_mx(
+                    w1_codes[a, b][:, c0:c1].bitcast(FP8X4), w1_plane[a, b][:, c0:c1], flat[:, 4 * c0 : 4 * c1]
+                )
+
+        quantise_w1(0, 0, cast_w1(0, 0))
+        damping(0, 0, after="w1_raw000")
         damping(1, 0)
-        damping(0, 1)
-        damping(1, 1)
+        for n in range(EARLY):
+            damping(n, 1)
 
         v_codes = [held(f"v_codes{a}", [P, S], U32, on="w3_bf0" if a == 0 else None) for a in range(2)]
         for a in range(2):
             nc.vector.tensor_copy(v_codes[a][:], tab_win[a][:].bitcast(U32).indirect(lists[:]))
 
-        load_w1(1, 1, "tab_win0", "tab_win1")
+        load_w1(1, 1, "tab2_swin", "tab_win0")
 
         w2_codes = held("w2_codes", [P, H], I32)
         w2_plane = held("w2_plane", [P, H], U8, on="v_picked")
@@ -181,35 +205,13 @@ def tile_list_cue_break_scores_kernel(
         w4_codes = held("w4_codes", [P, 2, 2 * N], U8, on="w2_raw")
         nc.sync.dma_start(w4_codes[:].bitcast(I32), w4_words.rearrange("a p c -> p a c").bitcast(I32))
 
-        w1_codes, w1_plane = {}, {}
-
-        def quantise_w1(a, b):
-            w1_bf = held(f"w1_bf{a}{b}", [P, 4, P, 4], BF16)
-            dst = w1_bf[:].rearrange("p t m j -> p m j t")
-            parts = len(w1_raw[a, b])
-            for u in range(parts):
-                m = slice(P // parts * u, P // parts * (u + 1))
-                src = w1_raw[a, b][u][:].rearrange("p j (m t) -> p m j t", t=4)
-                if (a, b) == (0, 1):
-                    nc.scalar.activation(dst[:, m], src, ACT.Copy, scale=-1.0)
-                else:
-                    nc.vector.tensor_scalar_mul(dst[:, m], src, -1.0)
-            w1_codes[a, b] = held(f"w1_codes{a}{b}", [P, PASS], U32)
-            w1_plane[a, b] = held(f"w1_plane{a}{b}", [P, PASS], U8)
-            flat = w1_bf[:].rearrange("p t m j -> p (t m j)")
-            for u in range(parts):
-                c0, c1 = PASS // parts * u, PASS // parts * (u + 1)
-                nc.vector.quantize_mx(
-                    w1_codes[a, b][:, c0:c1].bitcast(FP8X4), w1_plane[a, b][:, c0:c1], flat[:, 4 * c0 : 4 * c1]
-                )
-
         h_codes, h_plane = [], []
 
-        def first_stage(c, b):
+        def first_stage(c, b, banks):
             cols = slice(W * c, W * (c + 1))
             slots = held(f"slots{c}{b}", [P, 4, W], BF16)
             for pair in range(2):
-                acc = psum_h.tile([P, 2, W], F32, name="acc")
+                acc = psum.tile([P, 2, W], F32, name="acc", tag=banks)
                 for i in range(2):
                     m2 = slice(PASS * b + P * (2 * pair + i), PASS * b + P * (2 * pair + i + 1))
                     nc.tensor.matmul_mx(
@@ -240,7 +242,7 @@ def tile_list_cue_break_scores_kernel(
 
         def second_stage(c, n):
             j0, w = CHUNKS[c]
-            e = psum_e.tile([P, PASS], F32, name="e")
+            e = psum.tile([P, PASS], F32, name="e", tag="e")
             for i in range(PASS // w):
                 e_banks[c, n + i] = e[:, w * i : w * (i + 1)]
                 order = (0, 1) if c == 0 else (1, 0)
@@ -268,25 +270,26 @@ def tile_list_cue_break_scores_kernel(
             places = list3[:, j0 // 16 : (j0 + w) // 16]
             nc.vector.tensor_tensor(pages[n][:].indirect(places), ys[c, n][:], gains[:, j0 : j0 + w], MULT)
 
-        quantise_w1(0, 0)
-        load_w3(1, on="tab_swin")
+        load_w3(1, on="tab_win1")
         load_page(on="w2_sraw")
         gains = held("gains", [P, S], F32, on="w1_bf00")
         nc.sync.dma_start(gains[:], wgo)
-        quantise_w1(1, 0)
+        quantise_w1(1, 0, cast_w1(1, 0))
         load_page(on="tab2_win")
-        quantise_w1(0, 1)
+        upper = cast_w1(0, 1)
         load_page(on="tab2_swin")
-        quantise_w1(1, 1)
+        lower = cast_w1(1, 1)
+        quantise_w1(0, 1, upper)
+        quantise_w1(1, 1, lower)
         load_page(on="tab_win0")
         for b in range(2):
             h_codes.append(held(f"h_codes{b}", [P, S], U32, on="w1_bf11" if b == 0 else None))
             h_plane.append(held(f"h_plane{b}", [P, S], U8))
-        quantise_h(0, 0, first_stage(0, 0))
+        quantise_h(0, 0, first_stage(0, 0, "e"))
         quantise_w3(1)
-        quantise_h(0, 1, first_stage(0, 1))
-        damping(2, 0, after="slots01")
-        damping(3, 0)
+        quantise_h(0, 1, first_stage(0, 1, "h0"))
+        damping(2, 0, after="slots01", banks="h1")
+        damping(3, 0, after="slots01", banks="h1")
         ahead = {0: (1,), 1: (2, 3), 2: ()}
         for c in range(len(CHUNKS)):
             damped(c, 0)
@@ -297,8 +300,8 @@ def tile_list_cue_break_scores_kernel(
             if ahead[c]:
                 last = ahead[c][-1]
                 for h in ahead[c]:
-                    quantise_h(h, 0, first_stage(h, 0))
-                    woven = first_stage(h, 1)
+                    quantise_h(h, 0, first_stage(h, 0, "h0"))
+                    woven = first_stage(h, 1, "h1")
                     if h == last:
                         damped(c, 3, on=f"slots{last}1")
                     quantise_h(h, 1, woven)
@@ -306,7 +309,7 @@ def tile_list_cue_break_scores_kernel(
                 damped(c, 3)
             place(c, 3)
             if c == 1:
-                for n in (2, 3):
+                for n in range(EARLY, 4):
                     damping(n, 1)
         for n in range(4):
             nc.sync.dma_start(out[P * n : P * (n + 1), :], pages[n][:])

from contextlib import ExitStack

import concourse.mybir as mybir

T, S, T2, K, K2, H, N = 2048, 1024, 2048, 1024, 512, 1024, 512
FLOPS = 2 * S * (K * H + K2 * H + K2 * N + H * N)

F32 = mybir.dt.float32
BF16 = mybir.dt.bfloat16
I32 = mybir.dt.int32
U32 = mybir.dt.uint32
U16 = mybir.dt.uint16
U8 = mybir.dt.uint8
FP8X4 = mybir.dt.float8_e4m3fn_x4
FP4X4 = mybir.dt.float4_e2m1fn_x4
ACT = mybir.ActivationFunctionType
MULT = mybir.AluOpType.mult

P = 128
PASS = 512
CHUNKS = ((0, 256), (256, 256), (512, 512))
W = 256
SC = ((0, 0, 0),)
W3S = (0,)
EARLY = 2
VW = ((0, 1), (1, 0))


def tile_list_cue_break_scores_kernel(
    tc, tab_words, tab_scales, tab2_words, tab2_scales, offs, offs2, offs3, w1, b1,
    w2_words, w2_scales, w3, w4_words, w4_scales, wgo, page1, out,
):
    nc = tc.nc
    with ExitStack() as ctx:
        keep = ctx.enter_context(tc.tile_pool(name="keep", bufs=1))
        work = ctx.enter_context(tc.tile_pool(name="work", bufs=2))
        psum = ctx.enter_context(tc.psum_pool(name="psum", bufs=2))

        def held(name, shape, dtype, on=None):
            return keep.tile(shape, dtype, name=name, tag=on or name, align_bytes=64)

        def words_of(dram):
            return dram.rearrange("p c i -> p (c i)").bitcast(I32)

        lists = held("lists", [P, S // 16], U16)
        list2 = held("list2", [P, S // 16], U16)
        list3 = held("list3", [P, S // 16], U16)
        tab2_win = held("tab2_win", [P, T], I32)
        tab2_swin = held("tab2_swin", [P, T], U8)
        tab_swin = held("tab_swin", [P, T], U8)
        w2_sraw = held("w2_sraw", [P, H], U8)
        v_planes = held("v_planes", [P, S], U8)

        nc.vector.memset(tab_swin[:].bitcast(I32), 0)
        nc.vector.memset(tab2_swin[:].bitcast(I32), 0)
        nc.sync.dma_start(lists[:], offs)
        nc.sync.dma_start(list2[:], offs2)
        nc.sync.dma_start(list3[:], offs3)
        for a in range(2):
            for r in range(2):
                nc.sync.dma_start(tab_swin[4 * a + r : P : 16, :].bitcast(I32), tab_scales[a, r:16:2, :].bitcast(I32))
        nc.sync.dma_start(tab2_win[:], words_of(tab2_words[0]))
        for r in range(4):
            nc.sync.dma_start(tab2_swin[r:P:32, :].bitcast(I32), tab2_scales[0, r:16:4, :].bitcast(I32))
        w3_raw = {}

        def load_w3(u, on=None):
            w3_raw[u] = held(f"w3_raw{u}", [P, 4, N // 2], F32, on=on)
            nc.sync.dma_start(w3_raw[u][:], w3[:, N // 2 * u : N // 2 * (u + 1)].rearrange("(p j) c -> p j c", j=4))

        load_w3(0)
        nc.gpsimd.memset(w2_sraw[:].bitcast(I32), 0)
        for r in range(4):
            nc.gpsimd.dma_start(w2_sraw[r:P:32, :].bitcast(I32), w2_scales[0, r:16:4, :].bitcast(I32))
        bias = held("bias", [P, 2, 4], F32)
        nc.gpsimd.dma_start(bias[:], b1.rearrange("(b p t) -> p b t", b=2, t=4))
        w4_planes = held("w4_planes", [P, 2, N], U8)
        nc.gpsimd.memset(w4_planes[:].rearrange("p a c -> p (a c)").bitcast(I32), 0)
        for r in range(4):
            nc.gpsimd.dma_start(
                w4_planes[r:P:32, :, :].bitcast(I32), w4_scales[:, r:16:4, :].rearrange("a d c -> d a c").bitcast(I32)
            )

        w1_raw = {}

        def load_w1(a, b, *on):
            width = PASS // len(on)
            w1_raw[a, b] = []
            for u, tag in enumerate(on):
                w1_raw[a, b].append(held(f"w1_raw{a}{b}{u}", [P, 4, width], F32, on=tag))
                c0 = PASS * b + width * u
                rows = w1[PASS * a : PASS * (a + 1), c0 : c0 + width]
                nc.sync.dma_start(w1_raw[a, b][u][:], rows.rearrange("(p j) c -> p j c", j=4))

        load_w1(0, 0, None)
        tab_win = [held(f"tab_win{a}", [P, T], I32) for a in range(2)]
        nc.sync.dma_start(tab_win[0][:], words_of(tab_words[0]))
        nc.sync.dma_start(tab_win[1][:], words_of(tab_words[1]))

        v_picked = held("v_picked", [P, S], U8)
        nc.vector.tensor_copy(v_picked[:], tab_swin[:].indirect(lists[:]))
        nc.vector.tensor_copy(v_planes[:].bitcast(I32), v_picked[:].bitcast(I32))

        def move_rows(a):
            for r in range(2):
                nc.sync.dma_start(
                    v_planes[4 * a + 2 + r : P : 32, :].bitcast(I32), v_picked[16 + 4 * a + r : P : 32, :].bitcast(I32)
                )

        move_rows(0)
        w2_raw = held("w2_raw", [P, H], I32)
        nc.sync.dma_start(w2_raw[:], words_of(w2_words[0]))
        load_w1(1, 0, "tab_swin")
        move_rows(1)

        pages = []

        def load_page(on):
            n = len(pages)
            pages.append(held(f"page{n}", [P, T2], F32, on=on))
            nc.sync.dma_start(pages[n][:], page1[P * n : P * (n + 1), :])

        v2_codes = held("v2_codes", [P, S], U32)
        v2_plane = held("v2_plane", [P, S], U8)
        nc.vector.tensor_copy(v2_codes[:], tab2_win[:].bitcast(U32).indirect(list2[:]))
        nc.vector.tensor_copy(v2_plane[:], tab2_swin[:].indirect(list2[:]))

        w3_codes, w3_plane = {}, {}

        def quantise_w3(u):
            w3_bf = held(f"w3_bf{u}", [P, N // 2, 4], BF16)
            cast = nc.scalar.copy if u in W3S else nc.vector.tensor_copy
            cast(w3_bf[:].rearrange("p (c i) j -> p c j i", i=4), w3_raw[u][:].rearrange("p j (c i) -> p c j i", i=4))
            w3_codes[u] = held(f"w3_codes{u}", [P, N // 2], U32)
            w3_plane[u] = held(f"w3_plane{u}", [P, N // 2], U8)
            nc.vector.quantize_mx(w3_codes[u][:].bitcast(FP8X4), w3_plane[u][:], w3_bf[:].rearrange("p c j -> p (c j)"))

        quantise_w3(0)
        load_w1(0, 1, "tab2_win")

        damp = held("damp", [P, 4, S], F32)

        def damping(n, half, after=None, banks="q"):
            cols = slice(PASS * half, PASS * (half + 1))
            m = slice(P * (n % 2), P * (n % 2 + 1))
            q = psum.tile([P, PASS], F32, name="q", tag=banks)
            nc.tensor.matmul_mx(
                q[:], lhsT=w3_codes[n // 2][:, m].bitcast(FP8X4), lhsT_scale=w3_plane[n // 2][:, m],
                rhs=v2_codes[:, cols].bitcast(FP8X4), rhs_scale=v2_plane[:, cols], start=True, stop=True,
            )
            if after is None:
                size = work.tile([P, PASS], F32, name="size")
            else:
                size = held("size_held", [P, PASS], F32, on=after)
            nc.scalar.activation(size[:], q[:], ACT.Abs)
            root = work.tile([P, PASS], F32, name="root")
            nc.scalar.activation(root[:], size[:], ACT.Abs_reciprocal_sqrt, bias=1.0)
            nc.scalar.activation(damp[:, n, cols], root[:], ACT.Square)

        w1_codes, w1_plane = {}, {}

        def cast_w1(a, b):
            w1_bf = held(f"w1_bf{a}{b}", [P, 4, P, 4], BF16)
            dst = w1_bf[:].rearrange("p t m j -> p m j t")
            parts = len(w1_raw[a, b])
            for u in range(parts):
                m = slice(P // parts * u, P // parts * (u + 1))
                src = w1_raw[a, b][u][:].rearrange("p j (m t) -> p m j t", t=4)
                if (a, b, u) in SC:
                    nc.scalar.activation(dst[:, m], src, ACT.Copy, scale=-1.0)
                else:
                    nc.vector.tensor_scalar_mul(dst[:, m], src, -1.0)
            return w1_bf

        def quantise_w1(a, b, w1_bf, on=None):
            parts = len(w1_raw[a, b])
            w1_codes[a, b] = held(f"w1_codes{a}{b}", [P, PASS], U32, on=on)
            w1_plane[a, b] = held(f"w1_plane{a}{b}", [P, PASS], U8)
            flat = w1_bf[:].rearrange("p t m j -> p (t m j)")
            for u in range(parts):
                c0, c1 = PASS // parts * u, PASS // parts * (u + 1)
                nc.vector.quantize_mx(
                    w1_codes[a, b][:, c0:c1].bitcast(FP8X4), w1_plane[a, b][:, c0:c1], flat[:, 4 * c0 : 4 * c1]
                )

        quantise_w1(0, 0, cast_w1(0, 0))
        damping(0, 0, after="w1_raw000")
        damping(1, 0)
        for n in range(EARLY):
            damping(n, 1)

        v_codes = [held(f"v_codes{a}", [P, S], U32, on="w3_bf0" if a == 0 else None) for a in range(2)]
        for a in range(2):
            nc.vector.tensor_copy(v_codes[a][:], tab_win[a][:].bitcast(U32).indirect(lists[:]))

        load_w1(1, 1, "tab2_swin", "tab_win0")

        w2_codes = held("w2_codes", [P, H], I32)
        w2_plane = held("w2_plane", [P, H], U8, on="v_picked")
        for dealt, raw in ((w2_codes, w2_raw), (w2_plane, w2_sraw)):
            nc.vector.tensor_copy(
                dealt[:].rearrange("p (b t m) -> p b m t", b=2, t=4), raw[:].rearrange("p (b m t) -> p b m t", b=2, t=4)
            )

        w4_codes = held("w4_codes", [P, 2, 2 * N], U8, on="w2_raw")
        nc.sync.dma_start(w4_codes[:].bitcast(I32), w4_words.rearrange("a p c -> p a c").bitcast(I32))

        h_codes, h_plane = [], []

        def first_stage(c, b, banks):
            cols = slice(W * c, W * (c + 1))
            slots = held(f"slots{c}{b}", [P, 4, W], BF16)
            for pair in range(2):
                acc = psum.tile([P, 2, W], F32, name="acc", tag=banks)
                for i in range(2):
                    m2 = slice(PASS * b + P * (2 * pair + i), PASS * b + P * (2 * pair + i + 1))
                    nc.tensor.matmul_mx(
                        acc[:, i, :], lhsT=w2_codes[:, m2].bitcast(FP8X4), lhsT_scale=w2_plane[:, m2],
                        rhs=v2_codes[:, cols].bitcast(FP8X4), rhs_scale=v2_plane[:, cols], start=(i == 0), stop=False,
                    )
                for a in range(2):
                    for i in range(2):
                        m1 = slice(P * (2 * pair + i), P * (2 * pair + i + 1))
                        nc.tensor.matmul_mx(
                            acc[:, i, :], lhsT=w1_codes[a, b][:, m1].bitcast(FP8X4), lhsT_scale=w1_plane[a, b][:, m1],
                            rhs=v_codes[a][:, cols].bitcast(FP8X4), rhs_scale=v_planes[4 * a : P, cols],
                            start=False, stop=(a == 1 and i == 1),
                        )
                for i in range(2):
                    t = 2 * pair + i
                    nc.scalar.activation(slots[:, t, :], acc[:, i, :], ACT.Abs, bias=bias[:, b, t : t + 1], scale=-1.0)
            woven = work.tile([P, W, 4], BF16, name="woven", bufs=4, align_bytes=64)
            weave = nc.vector.tensor_copy if (c, b) in VW else nc.scalar.copy
            weave(woven[:].rearrange("p (c i) t -> p c t i", i=4), slots[:].rearrange("p t (c i) -> p c t i", i=4))
            return woven

        def quantise_h(c, b, woven):
            cols = slice(W * c, W * (c + 1))
            nc.vector.quantize_mx(h_codes[b][:, cols].bitcast(FP8X4), h_plane[b][:, cols], woven[:].rearrange("p c t -> p (c t)"))

        e_banks, ys = {}, {}

        def second_stage(c, n):
            j0, w = CHUNKS[c]
            e = psum.tile([P, PASS], F32, name="e", tag="e")
            for i in range(PASS // w):
                e_banks[c, n + i] = e[:, w * i : w * (i + 1)]
                order = (0, 1) if c == 0 else (1, 0)
                for b in order:
                    nc.tensor.matmul_mx(
                        e_banks[c, n + i],
                        lhsT=w4_codes[:, b, 2 * P * (n + i) : 2 * P * (n + i + 1)].bitcast(FP4X4),
                        lhsT_scale=w4_planes[:, b, P * (n + i) : P * (n + i + 1)],
                        rhs=h_codes[b][:, j0 : j0 + w].bitcast(FP8X4), rhs_scale=h_plane[b][:, j0 : j0 + w],
                        start=(b == order[0]), stop=(b == order[1]),
                    )

        def damped(c, n, on=None):
            j0, w = CHUNKS[c]
            if n % (PASS // w) == 0:
                second_stage(c, n)
            if on is None:
                ys[c, n] = work.tile([P, w], F32, name="y", bufs=3)
            else:
                ys[c, n] = held("y_held", [P, w], F32, on=on)
            nc.vector.tensor_tensor(ys[c, n][:], e_banks[c, n], damp[:, n, j0 : j0 + w], MULT)

        def place(c, n):
            j0, w = CHUNKS[c]
            places = list3[:, j0 // 16 : (j0 + w) // 16]
            nc.vector.tensor_tensor(pages[n][:].indirect(places), ys[c, n][:], gains[:, j0 : j0 + w], MULT)

        load_w3(1, on="tab_win1")
        load_page(on="w2_sraw")
        gains = held("gains", [P, S], F32, on="w1_bf00")
        nc.sync.dma_start(gains[:], wgo)
        quantise_w1(1, 0, cast_w1(1, 0))
        load_page(on="tab2_win")
        upper = cast_w1(0, 1)
        load_page(on="tab2_swin")
        lower = cast_w1(1, 1)
        quantise_w1(0, 1, upper)
        quantise_w1(1, 1, lower)
        load_page(on="tab_win0")
        for b in range(2):
            h_codes.append(held(f"h_codes{b}", [P, S], U32, on="w1_bf11" if b == 0 else None))
            h_plane.append(held(f"h_plane{b}", [P, S], U8))
        quantise_h(0, 0, first_stage(0, 0, "e"))
        quantise_w3(1)
        quantise_h(0, 1, first_stage(0, 1, "h0"))
        damping(2, 0, after="slots01", banks="h1")
        damping(3, 0, after="slots01", banks="h1")
        ahead = {0: (1,), 1: (2, 3), 2: ()}
        for c in range(len(CHUNKS)):
            damped(c, 0)
            for n in range(3):
                if n < 2:
                    damped(c, n + 1)
                place(c, n)
            if ahead[c]:
                last = ahead[c][-1]
                for h in ahead[c]:
                    quantise_h(h, 0, first_stage(h, 0, "h0"))
                    woven = first_stage(h, 1, "h1")
                    if h == last:
                        damped(c, 3, on=f"slots{last}1")
                    quantise_h(h, 1, woven)
            else:
                damped(c, 3)
            place(c, 3)
            if c == 1:
                for n in range(EARLY, 4):
                    damping(n, 1)
        for n in range(4):
            nc.sync.dma_start(out[P * n : P * (n + 1), :], pages[n][:])
